import numpy as np
import ml_dtypes


def mxq(x, axis, fmt="e4m3"):
    dtype, down = {"e4m3": (ml_dtypes.float8_e4m3fn, 7), "e5m2": (ml_dtypes.float8_e5m2, 14)}[fmt]
    v = np.moveaxis(np.asarray(x, np.float32).astype(ml_dtypes.bfloat16).astype(np.float64), axis, -1)
    blocks = v.reshape(v.shape[:-1] + (-1, 32))
    amax = np.abs(blocks).max(-1, keepdims=True)
    byte = np.maximum(np.where(amax > 0, np.frexp(amax)[1] - 1 + 127, 0) - down, 1)
    scale = np.exp2(byte - 127.0)
    codes = (blocks / scale).astype(np.float32).astype(dtype).astype(np.float64)
    return np.moveaxis((codes * scale).reshape(v.shape), -1, axis)


WIDE = False


def mx_kscale(k):
    if not WIDE:
        return np.ones(k)
    levels = np.array([10, -10, 5, -5, 0])
    if k % 512:
        return np.exp2(np.random.permutation(np.resize(levels, k // 32))).repeat(32)
    a = np.empty((k // 512, 16))
    for p in range(k // 512):
        a[p, :8] = np.random.permutation(np.resize(levels, 8))
        for g in range(8):
            far = levels[np.abs(levels - a[p, g]) >= 10]
            a[p, g + 8] = far[np.random.randint(len(far))]
    return np.exp2(a.ravel()).repeat(32)


def f64(x):
    return np.asarray(x).astype(np.float64)


def striped(idx):
    return np.tile(np.asarray(idx).reshape(-1, 16).T, (8, 1)).astype(np.uint16)


def unstriped(offs):
    return offs[:16].T.reshape(-1).astype(np.int64)


E2M1 = np.array([0.0, 0.5, 1.0, 1.5, 2.0, 3.0, 4.0, 6.0, -0.0, -0.5, -1.0, -1.5, -2.0, -3.0, -4.0, -6.0])


def pack_weight(w, fmt):
    k, n = w.shape
    w = f64(np.asarray(w, np.float32).astype(ml_dtypes.bfloat16)).reshape(k // 32, 32, n)
    amax = np.abs(w).max(1)
    if fmt == "e4m3":
        byte = np.frexp(amax)[1] - 1 + 127 - 7
    else:
        mant, ex = np.frexp(amax / 6.0)
        byte = np.where(mant > 0.5, ex, ex - 1) + 127
    byte = np.clip(np.where(amax > 0, byte, 1), 1, 254)
    scaled = (w * np.exp2(127.0 - byte)[:, None, :]).reshape(k, n).astype(np.float32)
    by_word = np.ascontiguousarray(scaled.reshape(k // 512, 128, 4, n).transpose(0, 1, 3, 2))
    if fmt == "e4m3":
        words = by_word.astype(ml_dtypes.float8_e4m3fn).view(np.uint8)
    else:
        c = by_word.astype(ml_dtypes.float4_e2m1fn).view(np.uint8) & 0xF
        words = (c[..., 0::2] | (c[..., 1::2] << 4)).reshape(k // 512, 128, 2 * n)
    return np.ascontiguousarray(words), np.ascontiguousarray(byte.astype(np.uint8).reshape(k // 512, 16, n))


def unpack_weight(words, scales, fmt):
    g, _, n = scales.shape
    words = np.ascontiguousarray(words).reshape(g, 128, n, -1)
    if fmt == "e4m3":
        vals = words.view(ml_dtypes.float8_e4m3fn).astype(np.float64)
    else:
        nib = np.empty((g, 128, n, 4), np.uint8)
        nib[..., 0::2] = words & 0xF
        nib[..., 1::2] = words >> 4
        vals = E2M1[nib]
    vals = vals * np.repeat(np.exp2(scales.astype(np.float64) - 127.0), 8, axis=1)[..., None]
    return vals.transpose(0, 1, 3, 2).reshape(g * 512, n)


def softplus(v):
    return np.log(1.0 + np.exp(v))


def sigmoid(v):
    return 1.0 / (1.0 + np.exp(-v))


def bf(x):
    return np.asarray(x, np.float32).astype(ml_dtypes.bfloat16)


def planes(Y):
    r, m = Y.shape
    b = f64(bf(Y)).reshape(r // 32, 32, m)
    amax = np.abs(b).max(1)
    byte = np.clip(np.where(amax > 0, np.frexp(amax)[1] - 1 + 127 - 7, 1), 1, 254)
    codes = (b * np.exp2(127.0 - byte)[:, None, :]).reshape(r, m).astype(np.float32).astype(ml_dtypes.float8_e4m3fn).view(np.uint8)
    words = codes.reshape(r // 512, 128, 4, m).transpose(0, 1, 3, 2)
    return np.ascontiguousarray(words), np.ascontiguousarray(byte.astype(np.uint8).reshape(r // 512, 16, m))


K, R, F, T, J, M = 512, 512, 512, 2048, 512, 256


def setup_inputs():
    n = np.random.standard_normal
    idx = np.random.permutation(T)[:J]
    idx2 = np.random.permutation(J)[:M]
    idx3 = np.random.permutation(J)[:M]
    idx4 = np.random.permutation(J)[:M]
    fk = mx_kscale(K)
    fr = mx_kscale(R)
    dtabp = pack_weight(n((K, T)) / fk[:, None], "e4m3")
    tabp = pack_weight(n((K, T)) / fk[:, None], "e4m3")
    return {
        "dtab_words": dtabp[0],
        "dtab_scales": dtabp[1],
        "tab_words": tabp[0],
        "tab_scales": tabp[1],
        "w1": (n((K, R)) * 1 / np.sqrt(K) * fk[:, None]).astype(np.float32),
        "bias": (np.random.uniform(-0.5, 0.5, (R, 1))).astype(np.float32),
        "rs": (np.random.uniform(0.5, 2.0, (R, 1)) * fr[:, None]).astype(np.float32),
        "wor": (n((R, F)) * 1 / np.sqrt(R) / fr[:, None]).astype(np.float32),
        "res": (n((F, M)) * 0.5).astype(np.float32),
        "offs": striped(idx),
        "offs2": striped(idx2),
        "offs3": striped(idx3),
        "offs4": striped(idx4),
    }


def reference(dtab_words, dtab_scales, tab_words, tab_scales, w1, bias, rs, wor, res, offs, offs2, offs3, offs4):
    idx = unstriped(offs)
    idx2 = unstriped(offs2)
    idx3 = unstriped(offs3)
    idx4 = unstriped(offs4)
    dtabu = unpack_weight(dtab_words, dtab_scales, "e4m3")
    tabu = unpack_weight(tab_words, tab_scales, "e4m3")
    w1q = mxq(f64(w1), 0, "e4m3")
    tabidxg = tabu[:, idx]
    a = w1q.T @ tabidxg
    dtabidxg = dtabu[:, idx]
    ta = w1q.T @ dtabidxg
    h1 = softplus(a + f64(bias))
    s = h1[:, idx2] * h1[:, idx3] * h1[:, idx4]
    th1 = ta * sigmoid(a + f64(bias))
    ts = (th1[:, idx2] * h1[:, idx3] + th1[:, idx3] * h1[:, idx2]) * h1[:, idx4] + th1[:, idx4] * h1[:, idx2] * h1[:, idx3]
    tu1 = ts / (s + 1.0)
    fo1 = tu1 * f64(rs)
    worq = mxq(f64(wor), 0, "e4m3")
    fo1q = mxq(fo1, 0, "e4m3")
    yo = worq.T @ fo1q
    y = yo + f64(res)
    words, scales = planes(y)
    return y, words, scales

@@ -1,0 +1,220 @@
+from contextlib import ExitStack
+
+import concourse.mybir as mybir
+
+K, R, F, T, J, M = 512, 512, 512, 2048, 512, 256
+FLOPS = 2 * (2 * K * R * J + R * F * M)
+
+F32 = mybir.dt.float32
+BF16 = mybir.dt.bfloat16
+I32 = mybir.dt.int32
+U32 = mybir.dt.uint32
+U16 = mybir.dt.uint16
+U8 = mybir.dt.uint8
+FP8X4 = mybir.dt.float8_e4m3fn_x4
+ALU = mybir.AluOpType
+ACT = mybir.ActivationFunctionType
+
+P = 128
+PACK = 4
+TINY = 1e-19
+
+
+def tile_attend_ttriples_o_pl_kernel(tc, dtab_words, dtab_scales, tab_words, tab_scales, w1, bias, rs, wor, res,
+                                      offs, offs2, offs3, offs4, out_0, out_1, out_2):
+    nc = tc.nc
+    with ExitStack() as ctx:
+        lists = ctx.enter_context(tc.tile_pool(name="lists", bufs=1))
+        keep = ctx.enter_context(tc.tile_pool(name="keep", bufs=1))
+        psum = ctx.enter_context(tc.psum_pool(name="psum", bufs=4))
+
+        def sb(shape, dtype, name, tag=None):
+            return keep.tile(shape, dtype, name=name, tag=tag or name, align_bytes=64)
+
+        def words_view(ap):
+            return ap[0].rearrange("p n t -> p (n t)").bitcast(I32)
+
+        def load_scales(queue, tile, src):
+            for q in range(4):
+                queue.dma_start(out=tile[32 * q:32 * q + 4, :].bitcast(I32), in_=src[0, 4 * q:4 * q + 4, :].bitcast(I32))
+
+        warm = sb([P, 1], F32, "warm")
+        warm2 = sb([P, 1], F32, "warm2")
+        nc.vector.memset(warm[:], 0.0)
+        nc.scalar.activation(out=warm2[:], in_=warm[:], func=ACT.Sigmoid)
+
+        tab_s = sb([P, T], U8, "tab_s")
+        dtab_s = sb([P, T], U8, "dtab_s")
+        nc.gpsimd.memset(dtab_s[:].bitcast(I32), 0)
+
+        o1 = lists.tile([P, J // 16], U16, name="o1")
+        o2 = lists.tile([P, M // 16], U16, name="o2")
+        o3 = lists.tile([P, M // 16], U16, name="o3")
+        o4 = lists.tile([P, M // 16], U16, name="o4")
+        tab_w = sb([P, T], I32, "tab_w")
+        dtab_w = sb([P, T], I32, "dtab_w")
+        HALF = R // 2
+        w1_raw = [sb([P, PACK, HALF], F32, "w1_raw%d" % h) for h in range(2)]
+        wor_raw = sb([P, PACK, F], F32, "wor_raw")
+        res_sb = sb([P, PACK, M], F32, "res_sb")
+        bias_sb = sb([P, PACK], F32, "bias_sb")
+        rs_sb = sb([P, PACK], F32, "rs_sb")
+
+        nc.sync.dma_start(o1[:], offs)
+        for q in range(4):
+            rows = tab_scales[0, 4 * q:4 * q + 4, :].bitcast(I32)
+            nc.sync.dma_start(out=tab_s[32 * q:32 * q + 32, :].bitcast(I32), in_=rows.unsqueeze(0).broadcast_to([8, 4, T // 4]))
+        w1_v = w1.rearrange("(p j) r -> p j r", j=PACK)
+        nc.sync.dma_start(out=w1_raw[0][:], in_=w1_v[:, :, :HALF])
+        nc.sync.dma_start(out=tab_w[:], in_=words_view(tab_words))
+        nc.sync.dma_start(out=w1_raw[1][:], in_=w1_v[:, :, HALF:])
+        nc.sync.dma_start(out=bias_sb[:], in_=bias.rearrange("(p t) o -> p (t o)", t=PACK))
+        load_scales(nc.sync, dtab_s, dtab_scales)
+        nc.sync.dma_start(out=dtab_w[:], in_=words_view(dtab_words))
+        nc.sync.dma_start(o2[:], offs2)
+        nc.sync.dma_start(o3[:], offs3)
+        nc.sync.dma_start(o4[:], offs4)
+        nc.sync.dma_start(out=rs_sb[:], in_=rs.rearrange("(p t) o -> p (t o)", t=PACK))
+        nc.sync.dma_start(out=wor_raw[:], in_=wor.rearrange("(p j) f -> p j f", j=PACK))
+        nc.sync.dma_start(out=res_sb[:], in_=res.rearrange("(p t) m -> p t m", t=PACK))
+
+        tabg_s = sb([P, J], U8, "tabg_s")
+        nc.vector.tensor_copy(tabg_s[:], tab_s[:].indirect(o1[:]))
+        tabg_w = sb([P, J], U32, "tabg_w", tag="tab_s")
+        nc.vector.tensor_copy(tabg_w[:], tab_w[:].bitcast(U32).indirect(o1[:]))
+
+        def deal(engine_copy, dst, raw, m0, m1, m_off):
+            engine_copy(
+                out=dst[:].rearrange("p t m j -> p m t j")[:, m0:m1],
+                in_=raw[:].rearrange("p j (m t) -> p m t j", t=PACK)[:, m0 - m_off:m1 - m_off],
+            )
+
+        w1_bf = sb([P, PACK, P, PACK], BF16, "w1_bf")
+        w1_q = sb([P, R], U32, "w1_q")
+        w1_s = sb([P, R], U8, "w1_s")
+
+        def quantise_w1(h):
+            for t in range(PACK):
+                cols = slice(t * P + 64 * h, t * P + 64 * h + 64)
+                nc.vector.quantize_mx(out=w1_q[:, cols].bitcast(FP8X4), scales=w1_s[:, cols],
+                                      in_=w1_bf[:, t, 64 * h:64 * h + 64, :].rearrange("p m j -> p (m j)"))
+
+        deal(nc.scalar.copy, w1_bf, w1_raw[0], 0, 64, 0)
+        quantise_w1(0)
+        deal(nc.scalar.copy, w1_bf, w1_raw[1], 64, 88, 64)
+        deal(nc.vector.tensor_copy, w1_bf, w1_raw[1], 88, 128, 64)
+        quantise_w1(1)
+
+        nbias = sb([P, PACK], F32, "nbias")
+        nc.vector.tensor_scalar(nbias[:], bias_sb[:], -1.0, None, ALU.mult)
+
+        def mm(out, lq, ls, cols, rq, rsc):
+            nc.tensor.matmul_mx(out=out, lhsT=lq[:, cols].bitcast(FP8X4), lhsT_scale=ls[:, cols],
+                                rhs=rq.bitcast(FP8X4), rhs_scale=rsc, start=True, stop=True)
+
+        a_ps = []
+        for t in range(PACK):
+            a_t = psum.tile([P, J], F32, name="a_ps", tag="a")
+            mm(a_t[:], w1_q, w1_s, slice(t * P, (t + 1) * P), tabg_w[:], tabg_s[:])
+            a_ps.append(a_t)
+
+        dtabg_s = sb([P, J], U8, "dtabg_s", tag="w1_bf")
+        nc.vector.tensor_copy(dtabg_s[:], dtab_s[:].indirect(o1[:]))
+        dtabg_w = sb([P, J], U32, "dtabg_w", tag="dtab_s")
+        nc.vector.tensor_copy(dtabg_w[:], dtab_w[:].bitcast(U32).indirect(o1[:]))
+        ta_ps = []
+        for t in range(PACK):
+            ta_t = psum.tile([P, J], F32, name="ta_ps", tag="ta")
+            mm(ta_t[:], w1_q, w1_s, slice(t * P, (t + 1) * P), dtabg_w[:], dtabg_s[:])
+            ta_ps.append(ta_t)
+
+        sn = [sb([P, J], F32, "sn%d" % t) for t in range(PACK)]
+        sp = [sb([P, J], F32, "sp%d" % t) for t in range(PACK)]
+        nl = [sb([P, J], F32, "nl%d" % t) for t in range(PACK)]
+        x = [sb([P, J], F32, "x%d" % t) for t in range(PACK)]
+        h1 = [sb([P, J], F32, "h1_%d" % t) for t in range(PACK)]
+        th1 = [sb([P, J], F32, "th1_%d" % t) for t in range(PACK)]
+        for t in range(PACK):
+            nc.scalar.activation(out=sn[t][:], in_=a_ps[t][:], func=ACT.Sigmoid, bias=nbias[:, t:t + 1], scale=-1.0)
+        for t in range(2):
+            nc.vector.tensor_scalar(x[t][:], a_ps[t][:], bias_sb[:, t:t + 1], None, ALU.add)
+        for t in range(PACK):
+            nc.gpsimd.tensor_scalar(sp[t][:], sn[t][:], -1.0, 1.0, ALU.mult, ALU.add)
+        for t in range(PACK):
+            nc.scalar.activation(out=nl[t][:], in_=sn[t][:], func=ACT.Ln, bias=TINY)
+            if t >= 2:
+                nc.scalar.activation(out=x[t][:], in_=a_ps[t][:], func=ACT.Identity, bias=bias_sb[:, t:t + 1])
+        for t in range(PACK):
+            nc.vector.tensor_tensor(th1[t][:], ta_ps[t][:], sp[t][:], ALU.mult)
+
+        wor_bf = sb([P, PACK, P, PACK], BF16, "wor_bf")
+        deal(nc.scalar.copy, wor_bf, wor_raw, 0, 128, 0)
+        wor_q = sb([P, F], U32, "wor_q")
+        wor_s = sb([P, F], U8, "wor_s")
+
+        h2 = sb([P, PACK, M], F32, "h2")
+        h3 = sb([P, PACK, M], F32, "h3")
+        h4 = sb([P, PACK, M], F32, "h4")
+        p23 = sb([P, PACK, M], F32, "p23")
+        s = sb([P, PACK, M], F32, "s")
+        for t in range(PACK):
+            nc.vector.scalar_tensor_tensor(h1[t][:], nl[t][:], -1.0, x[t][:], ALU.mult, ALU.max)
+            nc.vector.tensor_copy(h2[:, t, :], h1[t][:].indirect(o2[:]))
+            nc.vector.tensor_copy(h3[:, t, :], h1[t][:].indirect(o3[:]))
+            nc.vector.tensor_copy(h4[:, t, :], h1[t][:].indirect(o4[:]))
+            nc.vector.tensor_tensor(p23[:, t, :], h2[:, t, :], h3[:, t, :], ALU.mult)
+            nc.vector.tensor_tensor(s[:, t, :], p23[:, t, :], h4[:, t, :], ALU.mult)
+        nc.vector.quantize_mx(out=wor_q[:].bitcast(FP8X4), scales=wor_s[:], in_=wor_bf[:].rearrange("p t m j -> p (t m j)"))
+
+        lg = sb([P, PACK, M], F32, "lg")
+        rec = sb([P, PACK, M], F32, "rec")
+        nc.scalar.activation(out=lg[:], in_=s[:], func=ACT.Ln, bias=1.0)
+        nc.scalar.activation(out=rec[:], in_=lg[:], func=ACT.Exp, scale=-1.0)
+
+        ua = sb([P, PACK, M], F32, "ua")
+        ub = sb([P, PACK, M], F32, "ub")
+        uc = sb([P, PACK, M], F32, "uc")
+        uq = sb([P, PACK, M], F32, "uq")
+        ud = sb([P, PACK, M], F32, "ud")
+        ts = sb([P, PACK, M], F32, "ts")
+        fo = sb([P, PACK, M], F32, "fo")
+        for t in range(PACK):
+            nc.vector.tensor_tensor(ua[:, t, :], th1[t][:].indirect(o2[:]), h3[:, t, :], ALU.mult)
+            nc.vector.tensor_tensor(ub[:, t, :], th1[t][:].indirect(o3[:]), h2[:, t, :], ALU.mult)
+            nc.vector.tensor_tensor(uc[:, t, :], th1[t][:].indirect(o4[:]), p23[:, t, :], ALU.mult)
+            nc.vector.tensor_tensor(uq[:, t, :], ua[:, t, :], ub[:, t, :], ALU.add)
+            nc.vector.tensor_tensor(ud[:, t, :], uq[:, t, :], h4[:, t, :], ALU.mult)
+            nc.vector.tensor_tensor(ts[:, t, :], ud[:, t, :], uc[:, t, :], ALU.add)
+            nc.vector.scalar_tensor_tensor(fo[:, t, :], ts[:, t, :], rs_sb[:, t:t + 1], rec[:, t, :], ALU.mult, ALU.mult)
+
+        SPLIT = 96
+
+        def weave(dst, src):
+            view = src[:].rearrange("p t m -> p m t")
+            nc.scalar.copy(out=dst[:, :SPLIT, :], in_=view[:, :SPLIT, :])
+            nc.vector.tensor_copy(out=dst[:, SPLIT:, :], in_=view[:, SPLIT:, :])
+
+        fo_bf = sb([P, M, PACK], BF16, "fo_bf")
+        weave(fo_bf, fo)
+        fo_q = sb([P, M], U32, "fo_q")
+        fo_s = sb([P, M], U8, "fo_s")
+        nc.vector.quantize_mx(out=fo_q[:].bitcast(FP8X4), scales=fo_s[:], in_=fo_bf[:].rearrange("p m t -> p (m t)"))
+
+        y = sb([P, PACK, M], F32, "y")
+        out_v = out_0.rearrange("(p t) m -> p t m", t=PACK)
+        for t in range(PACK):
+            yo_t = psum.tile([P, M], F32, name="yo_ps", tag="a")
+            mm(yo_t[:], wor_q, wor_s, slice(t * P, (t + 1) * P), fo_q[:], fo_s[:])
+            nc.vector.tensor_tensor(y[:, t, :], yo_t[:], res_sb[:, t, :], ALU.add)
+            if t % 2:
+                nc.sync.dma_start(out=out_v[:, t - 1:t + 1, :], in_=y[:, t - 1:t + 1, :])
+
+        y_bf = sb([P, M, PACK], BF16, "y_bf")
+        weave(y_bf, y)
+        y_q = sb([P, M], U32, "y_q")
+        y_s = sb([P, M], U8, "y_s")
+        nc.vector.quantize_mx(out=y_q[:].bitcast(FP8X4), scales=y_s[:], in_=y_bf[:].rearrange("p m t -> p (m t)"))
+        nc.sync.dma_start(out=words_view(out_1), in_=y_q[:].bitcast(I32))
+        for q in range(4):
+            queue = nc.scalar if q % 2 else nc.sync
+            queue.dma_start(out=out_2[0, 4 * q:4 * q + 4, :].bitcast(I32), in_=y_s[32 * q:32 * q + 4, :].bitcast(I32))

@@ -106,7 +106,7 @@ def tile_attend_ttriples_o_pl_kernel(tc, dtab_words, dtab_scales, tab_words, tab
         quantise_w1(1)
 
         nbias = sb([P, PACK], F32, "nbias")
-        nc.vector.tensor_scalar(nbias[:], bias_sb[:], -1.0, None, ALU.mult)
+        nc.scalar.activation(out=nbias[:], in_=bias_sb[:], func=ACT.Copy, scale=-1.0)
 
         def mm(out, lq, ls, cols, rq, rsc):
             nc.tensor.matmul_mx(out=out, lhsT=lq[:, cols].bitcast(FP8X4), lhsT_scale=ls[:, cols],
@@ -129,25 +129,23 @@ def tile_attend_ttriples_o_pl_kernel(tc, dtab_words, dtab_scales, tab_words, tab
             ta_ps.append(ta_t)
 
         sn = [sb([P, J], F32, "sn%d" % t) for t in range(PACK)]
-        sp = [sb([P, J], F32, "sp%d" % t) for t in range(PACK)]
+        early = sb([P, PACK, J], F32, "early", tag="dtab_w")
+        sp = [early[:, t, :] for t in range(PACK)]
         nl = [sb([P, J], F32, "nl%d" % t) for t in range(PACK)]
-        x = [sb([P, J], F32, "x%d" % t) for t in range(PACK)]
-        h1 = [sb([P, J], F32, "h1_%d" % t) for t in range(PACK)]
+        x = [sb([P, J], F32, "x%d" % t)[:] for t in range(PACK)]
         th1 = [sb([P, J], F32, "th1_%d" % t) for t in range(PACK)]
         for t in range(PACK):
             nc.scalar.activation(out=sn[t][:], in_=a_ps[t][:], func=ACT.Sigmoid, bias=nbias[:, t:t + 1], scale=-1.0)
-        for t in range(2):
-            nc.vector.tensor_scalar(x[t][:], a_ps[t][:], bias_sb[:, t:t + 1], None, ALU.add)
         for t in range(PACK):
-            nc.gpsimd.tensor_scalar(sp[t][:], sn[t][:], -1.0, 1.0, ALU.mult, ALU.add)
+            nc.vector.tensor_scalar(sp[t], sn[t][:], -1.0, 1.0, ALU.mult, ALU.add)
         for t in range(PACK):
             nc.scalar.activation(out=nl[t][:], in_=sn[t][:], func=ACT.Ln, bias=TINY)
-            if t >= 2:
-                nc.scalar.activation(out=x[t][:], in_=a_ps[t][:], func=ACT.Identity, bias=bias_sb[:, t:t + 1])
+            nc.scalar.activation(out=x[t], in_=nl[t][:], func=ACT.Copy, scale=-1.0)
         for t in range(PACK):
-            nc.vector.tensor_tensor(th1[t][:], ta_ps[t][:], sp[t][:], ALU.mult)
+            nc.vector.tensor_tensor(th1[t][:], ta_ps[t][:], sp[t], ALU.mult)
 
-        wor_bf = sb([P, PACK, P, PACK], BF16, "wor_bf")
+        h1 = [sb([P, J], F32, "h1_%d" % t, tag="dtab_w" if t == 0 else None) for t in range(PACK)]
+        wor_bf = sb([P, PACK, P, PACK], BF16, "wor_bf", tag="nl3")
         deal(nc.scalar.copy, wor_bf, wor_raw, 0, 128, 0)
         wor_q = sb([P, F], U32, "wor_q")
         wor_s = sb([P, F], U8, "wor_s")
@@ -157,19 +155,16 @@ def tile_attend_ttriples_o_pl_kernel(tc, dtab_words, dtab_scales, tab_words, tab
         h4 = sb([P, PACK, M], F32, "h4")
         p23 = sb([P, PACK, M], F32, "p23")
         s = sb([P, PACK, M], F32, "s")
+        def softplus(t):
+            nc.vector.scalar_tensor_tensor(h1[t][:], a_ps[t][:], bias_sb[:, t:t + 1], x[t], ALU.add, ALU.max)
+
+        softplus(0)
         for t in range(PACK):
-            nc.vector.scalar_tensor_tensor(h1[t][:], nl[t][:], -1.0, x[t][:], ALU.mult, ALU.max)
             nc.vector.tensor_copy(h2[:, t, :], h1[t][:].indirect(o2[:]))
             nc.vector.tensor_copy(h3[:, t, :], h1[t][:].indirect(o3[:]))
+            if t + 1 < PACK:
+                softplus(t + 1)
             nc.vector.tensor_copy(h4[:, t, :], h1[t][:].indirect(o4[:]))
-            nc.vector.tensor_tensor(p23[:, t, :], h2[:, t, :], h3[:, t, :], ALU.mult)
-            nc.vector.tensor_tensor(s[:, t, :], p23[:, t, :], h4[:, t, :], ALU.mult)
-        nc.vector.quantize_mx(out=wor_q[:].bitcast(FP8X4), scales=wor_s[:], in_=wor_bf[:].rearrange("p t m j -> p (t m j)"))
-
-        lg = sb([P, PACK, M], F32, "lg")
-        rec = sb([P, PACK, M], F32, "rec")
-        nc.scalar.activation(out=lg[:], in_=s[:], func=ACT.Ln, bias=1.0)
-        nc.scalar.activation(out=rec[:], in_=lg[:], func=ACT.Exp, scale=-1.0)
 
         ua = sb([P, PACK, M], F32, "ua")
         ub = sb([P, PACK, M], F32, "ub")
@@ -178,42 +173,70 @@ def tile_attend_ttriples_o_pl_kernel(tc, dtab_words, dtab_scales, tab_words, tab
         ud = sb([P, PACK, M], F32, "ud")
         ts = sb([P, PACK, M], F32, "ts")
         fo = sb([P, PACK, M], F32, "fo")
-        for t in range(PACK):
-            nc.vector.tensor_tensor(ua[:, t, :], th1[t][:].indirect(o2[:]), h3[:, t, :], ALU.mult)
-            nc.vector.tensor_tensor(ub[:, t, :], th1[t][:].indirect(o3[:]), h2[:, t, :], ALU.mult)
-            nc.vector.tensor_tensor(uc[:, t, :], th1[t][:].indirect(o4[:]), p23[:, t, :], ALU.mult)
-            nc.vector.tensor_tensor(uq[:, t, :], ua[:, t, :], ub[:, t, :], ALU.add)
-            nc.vector.tensor_tensor(ud[:, t, :], uq[:, t, :], h4[:, t, :], ALU.mult)
-            nc.vector.tensor_tensor(ts[:, t, :], ud[:, t, :], uc[:, t, :], ALU.add)
-            nc.vector.scalar_tensor_tensor(fo[:, t, :], ts[:, t, :], rs_sb[:, t:t + 1], rec[:, t, :], ALU.mult, ALU.mult)
+        lg = sb([P, PACK, M], F32, "lg")
+        rec = sb([P, PACK, M], F32, "rec")
+        recs = sb([P, PACK, M], F32, "recs")
 
-        SPLIT = 96
+        def fused(out, t, offsets, other):
+            nc.vector.tensor_tensor(out[:, t, :], th1[t][:].indirect(offsets[:]), other[:, t, :], ALU.mult)
+
+        nc.vector.tensor_tensor(p23[:], h2[:], h3[:], ALU.mult)
+        fused(ua, 0, o2, h3)
+        nc.vector.tensor_tensor(s[:], p23[:], h4[:], ALU.mult)
+        nc.scalar.activation(out=lg[:], in_=s[:], func=ACT.Ln, bias=1.0)
+        nc.scalar.activation(out=rec[:], in_=lg[:], func=ACT.Exp, scale=-1.0)
+        for t in range(PACK):
+            nc.scalar.activation(out=recs[:, t, :], in_=rec[:, t, :], func=ACT.Copy, scale=rs_sb[:, t:t + 1])
+        fused(ub, 0, o3, h2)
+        nc.vector.quantize_mx(out=wor_q[:].bitcast(FP8X4), scales=wor_s[:], in_=wor_bf[:].rearrange("p t m j -> p (t m j)"))
+        for t in range(1, PACK):
+            fused(ua, t, o2, h3)
+            fused(ub, t, o3, h2)
+        fused(uc, 0, o4, p23)
+        nc.vector.tensor_tensor(uq[:], ua[:], ub[:], ALU.add)
+        fused(uc, 1, o4, p23)
+        nc.vector.tensor_tensor(ud[:], uq[:], h4[:], ALU.mult)
+        fused(uc, 2, o4, p23)
+        fused(uc, 3, o4, p23)
+
+        HM = M // 2
+        halves = [slice(0, HM), slice(HM, M)]
+        weavers = [nc.scalar.copy, nc.vector.tensor_copy]
+        for cols in halves:
+            nc.vector.tensor_tensor(ts[:, :, cols], ud[:, :, cols], uc[:, :, cols], ALU.add)
+        for cols in halves:
+            nc.vector.tensor_tensor(fo[:, :, cols], ts[:, :, cols], recs[:, :, cols], ALU.mult)
 
         def weave(dst, src):
             view = src[:].rearrange("p t m -> p m t")
-            nc.scalar.copy(out=dst[:, :SPLIT, :], in_=view[:, :SPLIT, :])
-            nc.vector.tensor_copy(out=dst[:, SPLIT:, :], in_=view[:, SPLIT:, :])
+            for cols, copy in zip(halves, weavers):
+                copy(out=dst[:, cols, :], in_=view[:, cols, :])
+
+        def quantise_halves(codes, scales, src):
+            for cols in halves:
+                nc.vector.quantize_mx(out=codes[:, cols].bitcast(FP8X4), scales=scales[:, cols],
+                                      in_=src[:, cols, :].rearrange("p m t -> p (m t)"))
 
         fo_bf = sb([P, M, PACK], BF16, "fo_bf")
         weave(fo_bf, fo)
         fo_q = sb([P, M], U32, "fo_q")
         fo_s = sb([P, M], U8, "fo_s")
-        nc.vector.quantize_mx(out=fo_q[:].bitcast(FP8X4), scales=fo_s[:], in_=fo_bf[:].rearrange("p m t -> p (m t)"))
+        quantise_halves(fo_q, fo_s, fo_bf)
 
         y = sb([P, PACK, M], F32, "y")
         out_v = out_0.rearrange("(p t) m -> p t m", t=PACK)
-        for t in range(PACK):
-            yo_t = psum.tile([P, M], F32, name="yo_ps", tag="a")
-            mm(yo_t[:], wor_q, wor_s, slice(t * P, (t + 1) * P), fo_q[:], fo_s[:])
-            nc.vector.tensor_tensor(y[:, t, :], yo_t[:], res_sb[:, t, :], ALU.add)
-            if t % 2:
-                nc.sync.dma_start(out=out_v[:, t - 1:t + 1, :], in_=y[:, t - 1:t + 1, :])
+        for cols in halves:
+            yo = psum.tile([P, PACK, HM], F32, name="yo_ps", tag="a")
+            for t in range(PACK):
+                mm(yo[:, t, :], wor_q, wor_s, slice(t * P, (t + 1) * P), fo_q[:, cols], fo_s[:, cols])
+            nc.vector.tensor_tensor(y[:, :, cols], yo[:], res_sb[:, :, cols], ALU.add)
+            nc.sync.dma_start(out=out_v[:, :, cols], in_=y[:, :, cols])
 
         y_bf = sb([P, M, PACK], BF16, "y_bf")
         weave(y_bf, y)
         y_q = sb([P, M], U32, "y_q")
         y_s = sb([P, M], U8, "y_s")
-        nc.vector.quantize_mx(out=y_q[:].bitcast(FP8X4), scales=y_s[:], in_=y_bf[:].rearrange("p m t -> p (m t)"))
+        quantise_halves(y_q, y_s, y_bf)
         nc.sync.dma_start(out=words_view(out_1), in_=y_q[:].bitcast(I32))
         for q in range(4):
             queue = nc.scalar if q % 2 else nc.sync

@@ -1,6 +1,7 @@
 from contextlib import ExitStack
 
 import concourse.mybir as mybir
+from concourse.masks import make_identity
 
 K, R, F, T, J, M = 512, 512, 512, 2048, 512, 256
 FLOPS = 2 * (2 * K * R * J + R * F * M)
@@ -46,6 +47,9 @@ def tile_attend_ttriples_o_pl_kernel(tc, dtab_words, dtab_scales, tab_words, tab
         tab_s = sb([P, T], U8, "tab_s")
         dtab_s = sb([P, T], U8, "dtab_s")
         nc.gpsimd.memset(dtab_s[:].bitcast(I32), 0)
+
+        ident = sb([P, P], F32, "ident")
+        make_identity(nc, ident[:])
 
         o1 = lists.tile([P, J // 16], U16, name="o1")
         o2 = lists.tile([P, M // 16], U16, name="o2")
@@ -169,7 +173,6 @@ def tile_attend_ttriples_o_pl_kernel(tc, dtab_words, dtab_scales, tab_words, tab
         ua = sb([P, PACK, M], F32, "ua")
         ub = sb([P, PACK, M], F32, "ub")
         uc = sb([P, PACK, M], F32, "uc")
-        uq = sb([P, PACK, M], F32, "uq")
         ud = sb([P, PACK, M], F32, "ud")
         ts = sb([P, PACK, M], F32, "ts")
         fo = sb([P, PACK, M], F32, "fo")
@@ -185,19 +188,44 @@ def tile_attend_ttriples_o_pl_kernel(tc, dtab_words, dtab_scales, tab_words, tab
         nc.vector.tensor_tensor(s[:], p23[:], h4[:], ALU.mult)
         nc.scalar.activation(out=lg[:], in_=s[:], func=ACT.Ln, bias=1.0)
         nc.scalar.activation(out=rec[:], in_=lg[:], func=ACT.Exp, scale=-1.0)
-        for t in range(PACK):
-            nc.scalar.activation(out=recs[:, t, :], in_=rec[:, t, :], func=ACT.Copy, scale=rs_sb[:, t:t + 1])
+        uq = sb([P, PACK, M], F32, "uq", tag="lg")
+
+        def turned_sum(t):
+            qt_ps = psum.tile([P, 2, P], F32, name="qt_ps", tag="ta")
+            for b in range(2):
+                cols = slice(b * P, (b + 1) * P)
+                nc.tensor.matmul(qt_ps[:, b, :], lhsT=ua[:, t, cols], rhs=ident[:], is_transpose=True, start=True, stop=False)
+                nc.tensor.matmul(qt_ps[:, b, :], lhsT=ub[:, t, cols], rhs=ident[:], is_transpose=True, start=False, stop=True)
+            nc.scalar.copy(out=uq[:, t, :], in_=qt_ps[:].rearrange("p b r -> p (b r)"))
+
+        def turn_back(pair):
+            q_ps = psum.tile([P, 2, M], F32, name="q_ps", tag="a")
+            for i in range(2):
+                for b in range(2):
+                    cols = slice(b * P, (b + 1) * P)
+                    nc.tensor.transpose(q_ps[:, i, cols], uq[:, 2 * pair + i, cols], ident[:])
+            return q_ps
+
+        def times_h4(pair, q_ps):
+            tiles = slice(2 * pair, 2 * pair + 2)
+            nc.vector.tensor_tensor(ud[:, tiles, :], q_ps[:], h4[:, tiles, :], ALU.mult)
+
         fused(ub, 0, o3, h2)
+        turned_sum(0)
         nc.vector.quantize_mx(out=wor_q[:].bitcast(FP8X4), scales=wor_s[:], in_=wor_bf[:].rearrange("p t m j -> p (t m j)"))
         for t in range(1, PACK):
             fused(ua, t, o2, h3)
             fused(ub, t, o3, h2)
+            turned_sum(t)
+        for t in range(PACK):
+            nc.scalar.activation(out=recs[:, t, :], in_=rec[:, t, :], func=ACT.Copy, scale=rs_sb[:, t:t + 1])
+        q_back = [turn_back(pair) for pair in range(2)]
         fused(uc, 0, o4, p23)
-        nc.vector.tensor_tensor(uq[:], ua[:], ub[:], ALU.add)
         fused(uc, 1, o4, p23)
-        nc.vector.tensor_tensor(ud[:], uq[:], h4[:], ALU.mult)
         fused(uc, 2, o4, p23)
+        times_h4(0, q_back[0])
         fused(uc, 3, o4, p23)
+        times_h4(1, q_back[1])
 
         HM = M // 2
         halves = [slice(0, HM), slice(HM, M)]

@@ -18,7 +18,10 @@ ACT = mybir.ActivationFunctionType
 
 P = 128
 PACK = 4
-TINY = 1e-19
+QUAD = 32
+HALF_P = P // 2
+W1_SCALAR_SHARE = 24
+LN_FLOOR = 1e-19
 
 
 def tile_attend_ttriples_o_pl_kernel(tc, dtab_words, dtab_scales, tab_words, tab_scales, w1, bias, rs, wor, res,
@@ -27,22 +30,25 @@ def tile_attend_ttriples_o_pl_kernel(tc, dtab_words, dtab_scales, tab_words, tab
     with ExitStack() as ctx:
         lists = ctx.enter_context(tc.tile_pool(name="lists", bufs=1))
         keep = ctx.enter_context(tc.tile_pool(name="keep", bufs=1))
-        psum = ctx.enter_context(tc.psum_pool(name="psum", bufs=4))
+        psum = ctx.enter_context(tc.psum_pool(name="psum", bufs=PACK))
 
-        def sb(shape, dtype, name, tag=None):
-            return keep.tile(shape, dtype, name=name, tag=tag or name, align_bytes=64)
+        def sb(shape, dtype, name, after=None):
+            return keep.tile(shape, dtype, name=name, tag=after or name, align_bytes=64)
 
         def words_view(ap):
-            return ap[0].rearrange("p n t -> p (n t)").bitcast(I32)
+            return ap[0].rearrange("p n q -> p (n q)").bitcast(I32)
 
-        def load_scales(queue, tile, src):
-            for q in range(4):
-                queue.dma_start(out=tile[32 * q:32 * q + 4, :].bitcast(I32), in_=src[0, 4 * q:4 * q + 4, :].bitcast(I32))
+        def product(out, lhs_codes, lhs_scales, q, rhs_codes, rhs_scales):
+            cols = slice(q * P, (q + 1) * P)
+            nc.tensor.matmul_mx(out=out, lhsT=lhs_codes[:, cols].bitcast(FP8X4), lhsT_scale=lhs_scales[:, cols],
+                                rhs=rhs_codes.bitcast(FP8X4), rhs_scale=rhs_scales, start=True, stop=True)
 
-        warm = sb([P, 1], F32, "warm")
-        warm2 = sb([P, 1], F32, "warm2")
-        nc.vector.memset(warm[:], 0.0)
-        nc.scalar.activation(out=warm2[:], in_=warm[:], func=ACT.Sigmoid)
+        zero = sb([P, 1], F32, "zero")
+        half = sb([P, 1], F32, "half")
+        floor = sb([P, 1], F32, "floor")
+        nc.vector.memset(zero[:], 0.0)
+        nc.scalar.activation(out=half[:], in_=zero[:], func=ACT.Sigmoid)
+        nc.scalar.activation(out=floor[:], in_=half[:], func=ACT.Copy, scale=2.0 * LN_FLOOR)
 
         tab_s = sb([P, T], U8, "tab_s")
         dtab_s = sb([P, T], U8, "dtab_s")
@@ -57,193 +63,186 @@ def tile_attend_ttriples_o_pl_kernel(tc, dtab_words, dtab_scales, tab_words, tab
         o4 = lists.tile([P, M // 16], U16, name="o4")
         tab_w = sb([P, T], I32, "tab_w")
         dtab_w = sb([P, T], I32, "dtab_w")
-        HALF = R // 2
-        w1_raw = [sb([P, PACK, HALF], F32, "w1_raw%d" % h) for h in range(2)]
+        w1_raw = [sb([P, PACK, R // 2], F32, "w1_raw%d" % h) for h in range(2)]
         wor_raw = sb([P, PACK, F], F32, "wor_raw")
         res_sb = sb([P, PACK, M], F32, "res_sb")
         bias_sb = sb([P, PACK], F32, "bias_sb")
         rs_sb = sb([P, PACK], F32, "rs_sb")
 
         nc.sync.dma_start(o1[:], offs)
-        for q in range(4):
-            rows = tab_scales[0, 4 * q:4 * q + 4, :].bitcast(I32)
-            nc.sync.dma_start(out=tab_s[32 * q:32 * q + 32, :].bitcast(I32), in_=rows.unsqueeze(0).broadcast_to([8, 4, T // 4]))
-        w1_v = w1.rearrange("(p j) r -> p j r", j=PACK)
-        nc.sync.dma_start(out=w1_raw[0][:], in_=w1_v[:, :, :HALF])
+        for quad in range(P // QUAD):
+            rows = tab_scales[0, 4 * quad:4 * quad + 4, :].bitcast(I32)
+            nc.sync.dma_start(out=tab_s[QUAD * quad:QUAD * (quad + 1), :].bitcast(I32),
+                              in_=rows.unsqueeze(0).broadcast_to([QUAD // 4, 4, T // 4]))
+        w1_rows = w1.rearrange("(p q) r -> p q r", q=PACK)
+        nc.sync.dma_start(out=w1_raw[0][:], in_=w1_rows[:, :, :R // 2])
         nc.sync.dma_start(out=tab_w[:], in_=words_view(tab_words))
-        nc.sync.dma_start(out=w1_raw[1][:], in_=w1_v[:, :, HALF:])
-        nc.sync.dma_start(out=bias_sb[:], in_=bias.rearrange("(p t) o -> p (t o)", t=PACK))
-        load_scales(nc.sync, dtab_s, dtab_scales)
+        nc.sync.dma_start(out=w1_raw[1][:], in_=w1_rows[:, :, R // 2:])
+        nc.sync.dma_start(out=bias_sb[:], in_=bias.rearrange("(p q) o -> p (q o)", q=PACK))
         nc.sync.dma_start(out=dtab_w[:], in_=words_view(dtab_words))
+        for i in range(4):
+            nc.sync.dma_start(out=dtab_s[i:P:QUAD, :].bitcast(I32), in_=dtab_scales[0, i:16:4, :].bitcast(I32))
         nc.sync.dma_start(o2[:], offs2)
         nc.sync.dma_start(o3[:], offs3)
         nc.sync.dma_start(o4[:], offs4)
-        nc.sync.dma_start(out=rs_sb[:], in_=rs.rearrange("(p t) o -> p (t o)", t=PACK))
-        nc.sync.dma_start(out=wor_raw[:], in_=wor.rearrange("(p j) f -> p j f", j=PACK))
-        nc.sync.dma_start(out=res_sb[:], in_=res.rearrange("(p t) m -> p t m", t=PACK))
+        nc.sync.dma_start(out=rs_sb[:], in_=rs.rearrange("(p q) o -> p (q o)", q=PACK))
+        nc.sync.dma_start(out=wor_raw[:], in_=wor.rearrange("(p q) f -> p q f", q=PACK))
+        nc.sync.dma_start(out=res_sb[:], in_=res.rearrange("(p q) m -> p q m", q=PACK))
 
         tabg_s = sb([P, J], U8, "tabg_s")
         nc.vector.tensor_copy(tabg_s[:], tab_s[:].indirect(o1[:]))
-        tabg_w = sb([P, J], U32, "tabg_w", tag="tab_s")
+        tabg_w = sb([P, J], U32, "tabg_w", after="tab_s")
         nc.vector.tensor_copy(tabg_w[:], tab_w[:].bitcast(U32).indirect(o1[:]))
 
-        def deal(engine_copy, dst, raw, m0, m1, m_off):
-            engine_copy(
-                out=dst[:].rearrange("p t m j -> p m t j")[:, m0:m1],
-                in_=raw[:].rearrange("p j (m t) -> p m t j", t=PACK)[:, m0 - m_off:m1 - m_off],
-            )
+        def deal(copy, dst, raw, c0, c1, c_first):
+            copy(out=dst[:].rearrange("p q c j -> p c q j")[:, c0:c1],
+                 in_=raw[:].rearrange("p j (c q) -> p c q j", q=PACK)[:, c0 - c_first:c1 - c_first])
 
         w1_bf = sb([P, PACK, P, PACK], BF16, "w1_bf")
         w1_q = sb([P, R], U32, "w1_q")
         w1_s = sb([P, R], U8, "w1_s")
 
         def quantise_w1(h):
-            for t in range(PACK):
-                cols = slice(t * P + 64 * h, t * P + 64 * h + 64)
+            for q in range(PACK):
+                cols = slice(q * P + HALF_P * h, q * P + HALF_P * (h + 1))
                 nc.vector.quantize_mx(out=w1_q[:, cols].bitcast(FP8X4), scales=w1_s[:, cols],
-                                      in_=w1_bf[:, t, 64 * h:64 * h + 64, :].rearrange("p m j -> p (m j)"))
+                                      in_=w1_bf[:, q, HALF_P * h:HALF_P * (h + 1), :].rearrange("p c j -> p (c j)"))
 
-        deal(nc.scalar.copy, w1_bf, w1_raw[0], 0, 64, 0)
+        deal(nc.scalar.copy, w1_bf, w1_raw[0], 0, HALF_P, 0)
         quantise_w1(0)
-        deal(nc.scalar.copy, w1_bf, w1_raw[1], 64, 88, 64)
-        deal(nc.vector.tensor_copy, w1_bf, w1_raw[1], 88, 128, 64)
+        deal(nc.scalar.copy, w1_bf, w1_raw[1], HALF_P, HALF_P + W1_SCALAR_SHARE, HALF_P)
+        deal(nc.vector.tensor_copy, w1_bf, w1_raw[1], HALF_P + W1_SCALAR_SHARE, P, HALF_P)
         quantise_w1(1)
 
-        nbias = sb([P, PACK], F32, "nbias")
-        nc.scalar.activation(out=nbias[:], in_=bias_sb[:], func=ACT.Copy, scale=-1.0)
-
-        def mm(out, lq, ls, cols, rq, rsc):
-            nc.tensor.matmul_mx(out=out, lhsT=lq[:, cols].bitcast(FP8X4), lhsT_scale=ls[:, cols],
-                                rhs=rq.bitcast(FP8X4), rhs_scale=rsc, start=True, stop=True)
+        neg_bias = sb([P, PACK], F32, "neg_bias")
+        nc.scalar.activation(out=neg_bias[:], in_=bias_sb[:], func=ACT.Copy, scale=-1.0)
 
         a_ps = []
-        for t in range(PACK):
-            a_t = psum.tile([P, J], F32, name="a_ps", tag="a")
-            mm(a_t[:], w1_q, w1_s, slice(t * P, (t + 1) * P), tabg_w[:], tabg_s[:])
-            a_ps.append(a_t)
+        for q in range(PACK):
+            a_q = psum.tile([P, J], F32, name="a_ps", tag="a")
+            product(a_q[:], w1_q, w1_s, q, tabg_w[:], tabg_s[:])
+            a_ps.append(a_q)
 
-        dtabg_s = sb([P, J], U8, "dtabg_s", tag="w1_bf")
-        nc.vector.tensor_copy(dtabg_s[:], dtab_s[:].indirect(o1[:]))
-        dtabg_w = sb([P, J], U32, "dtabg_w", tag="dtab_s")
+        dtabg_w = sb([P, J], U32, "dtabg_w", after="w1_bf")
         nc.vector.tensor_copy(dtabg_w[:], dtab_w[:].bitcast(U32).indirect(o1[:]))
+        dtabg_s = sb([P, J], U8, "dtabg_s", after="dtab_w")
+        nc.vector.tensor_copy(dtabg_s[:], dtab_s[:].indirect(o1[:]))
         ta_ps = []
-        for t in range(PACK):
-            ta_t = psum.tile([P, J], F32, name="ta_ps", tag="ta")
-            mm(ta_t[:], w1_q, w1_s, slice(t * P, (t + 1) * P), dtabg_w[:], dtabg_s[:])
-            ta_ps.append(ta_t)
+        for q in range(PACK):
+            ta_q = psum.tile([P, J], F32, name="ta_ps", tag="ta")
+            product(ta_q[:], w1_q, w1_s, q, dtabg_w[:], dtabg_s[:])
+            ta_ps.append(ta_q)
 
-        sn = [sb([P, J], F32, "sn%d" % t) for t in range(PACK)]
-        early = sb([P, PACK, J], F32, "early", tag="dtab_w")
-        sp = [early[:, t, :] for t in range(PACK)]
-        nl = [sb([P, J], F32, "nl%d" % t) for t in range(PACK)]
-        x = [sb([P, J], F32, "x%d" % t)[:] for t in range(PACK)]
-        th1 = [sb([P, J], F32, "th1_%d" % t) for t in range(PACK)]
-        for t in range(PACK):
-            nc.scalar.activation(out=sn[t][:], in_=a_ps[t][:], func=ACT.Sigmoid, bias=nbias[:, t:t + 1], scale=-1.0)
-        for t in range(PACK):
-            nc.vector.tensor_scalar(sp[t], sn[t][:], -1.0, 1.0, ALU.mult, ALU.add)
-        for t in range(PACK):
-            nc.scalar.activation(out=nl[t][:], in_=sn[t][:], func=ACT.Ln, bias=TINY)
-            nc.scalar.activation(out=x[t], in_=nl[t][:], func=ACT.Copy, scale=-1.0)
-        for t in range(PACK):
-            nc.vector.tensor_tensor(th1[t][:], ta_ps[t][:], sp[t], ALU.mult)
+        sig_neg = [sb([P, J], F32, "sig_neg%d" % q) for q in range(PACK)]
+        sig = sb([P, PACK, J], F32, "sig", after="dtab_s")
+        ln_sig = [sb([P, J], F32, "ln_sig%d" % q) for q in range(PACK)]
+        soft = [sb([P, J], F32, "soft%d" % q) for q in range(PACK)]
+        th1 = [sb([P, J], F32, "th1_%d" % q) for q in range(PACK)]
+        for q in range(PACK):
+            nc.scalar.activation(out=sig_neg[q][:], in_=a_ps[q][:], func=ACT.Sigmoid, bias=neg_bias[:, q:q + 1], scale=-1.0)
+        for q in range(PACK):
+            nc.vector.tensor_scalar(sig[:, q, :], sig_neg[q][:], -1.0, 1.0, ALU.mult, ALU.add)
+        for q in range(PACK):
+            nc.scalar.activation(out=ln_sig[q][:], in_=sig_neg[q][:], func=ACT.Ln, bias=floor[:])
+            nc.scalar.activation(out=soft[q][:], in_=ln_sig[q][:], func=ACT.Copy, scale=-1.0)
+        for q in range(PACK):
+            nc.vector.tensor_tensor(th1[q][:], ta_ps[q][:], sig[:, q, :], ALU.mult)
 
-        h1 = [sb([P, J], F32, "h1_%d" % t, tag="dtab_w" if t == 0 else None) for t in range(PACK)]
-        wor_bf = sb([P, PACK, P, PACK], BF16, "wor_bf", tag="nl3")
-        deal(nc.scalar.copy, wor_bf, wor_raw, 0, 128, 0)
+        h1 = [sb([P, J], F32, "h1_%d" % q, after="dtab_s" if q == 0 else None) for q in range(PACK)]
+        wor_bf = sb([P, PACK, P, PACK], BF16, "wor_bf", after="ln_sig%d" % (PACK - 1))
+        deal(nc.scalar.copy, wor_bf, wor_raw, 0, P, 0)
         wor_q = sb([P, F], U32, "wor_q")
         wor_s = sb([P, F], U8, "wor_s")
 
         h2 = sb([P, PACK, M], F32, "h2")
         h3 = sb([P, PACK, M], F32, "h3")
         h4 = sb([P, PACK, M], F32, "h4")
-        p23 = sb([P, PACK, M], F32, "p23")
+        h23 = sb([P, PACK, M], F32, "h23")
         s = sb([P, PACK, M], F32, "s")
-        def softplus(t):
-            nc.vector.scalar_tensor_tensor(h1[t][:], a_ps[t][:], bias_sb[:, t:t + 1], x[t], ALU.add, ALU.max)
+
+        def softplus(q):
+            nc.vector.scalar_tensor_tensor(h1[q][:], a_ps[q][:], bias_sb[:, q:q + 1], soft[q][:], ALU.add, ALU.max)
 
         softplus(0)
-        for t in range(PACK):
-            nc.vector.tensor_copy(h2[:, t, :], h1[t][:].indirect(o2[:]))
-            nc.vector.tensor_copy(h3[:, t, :], h1[t][:].indirect(o3[:]))
-            if t + 1 < PACK:
-                softplus(t + 1)
-            nc.vector.tensor_copy(h4[:, t, :], h1[t][:].indirect(o4[:]))
+        for q in range(PACK):
+            nc.vector.tensor_copy(h2[:, q, :], h1[q][:].indirect(o2[:]))
+            nc.vector.tensor_copy(h3[:, q, :], h1[q][:].indirect(o3[:]))
+            if q + 1 < PACK:
+                softplus(q + 1)
+            nc.vector.tensor_copy(h4[:, q, :], h1[q][:].indirect(o4[:]))
 
-        ua = sb([P, PACK, M], F32, "ua")
-        ub = sb([P, PACK, M], F32, "ub")
-        uc = sb([P, PACK, M], F32, "uc")
-        ud = sb([P, PACK, M], F32, "ud")
+        th2_h3 = sb([P, PACK, M], F32, "th2_h3")
+        th3_h2 = sb([P, PACK, M], F32, "th3_h2")
+        th4_h23 = sb([P, PACK, M], F32, "th4_h23")
+        pair_h4 = sb([P, PACK, M], F32, "pair_h4")
         ts = sb([P, PACK, M], F32, "ts")
         fo = sb([P, PACK, M], F32, "fo")
-        lg = sb([P, PACK, M], F32, "lg")
+        ln_den = sb([P, PACK, M], F32, "ln_den")
         rec = sb([P, PACK, M], F32, "rec")
-        recs = sb([P, PACK, M], F32, "recs")
+        rec_rs = sb([P, PACK, M], F32, "rec_rs")
 
-        def fused(out, t, offsets, other):
-            nc.vector.tensor_tensor(out[:, t, :], th1[t][:].indirect(offsets[:]), other[:, t, :], ALU.mult)
+        def th_times(out, q, offsets, other):
+            nc.vector.tensor_tensor(out[:, q, :], th1[q][:].indirect(offsets[:]), other[:, q, :], ALU.mult)
 
-        nc.vector.tensor_tensor(p23[:], h2[:], h3[:], ALU.mult)
-        fused(ua, 0, o2, h3)
-        nc.vector.tensor_tensor(s[:], p23[:], h4[:], ALU.mult)
-        nc.scalar.activation(out=lg[:], in_=s[:], func=ACT.Ln, bias=1.0)
-        nc.scalar.activation(out=rec[:], in_=lg[:], func=ACT.Exp, scale=-1.0)
-        uq = sb([P, PACK, M], F32, "uq", tag="lg")
+        nc.vector.tensor_tensor(h23[:], h2[:], h3[:], ALU.mult)
+        th_times(th2_h3, 0, o2, h3)
+        nc.vector.tensor_tensor(s[:], h23[:], h4[:], ALU.mult)
+        nc.scalar.activation(out=ln_den[:], in_=s[:], func=ACT.Ln, bias=1.0)
+        nc.scalar.activation(out=rec[:], in_=ln_den[:], func=ACT.Exp, scale=-1.0)
 
-        def turned_sum(t):
-            qt_ps = psum.tile([P, 2, P], F32, name="qt_ps", tag="ta")
-            for b in range(2):
-                cols = slice(b * P, (b + 1) * P)
-                nc.tensor.matmul(qt_ps[:, b, :], lhsT=ua[:, t, cols], rhs=ident[:], is_transpose=True, start=True, stop=False)
-                nc.tensor.matmul(qt_ps[:, b, :], lhsT=ub[:, t, cols], rhs=ident[:], is_transpose=True, start=False, stop=True)
-            nc.scalar.copy(out=uq[:, t, :], in_=qt_ps[:].rearrange("p b r -> p (b r)"))
+        pair_turned = sb([P, PACK, M], F32, "pair_turned", after="ln_den")
+        blocks = [slice(b * P, (b + 1) * P) for b in range(M // P)]
 
-        def turn_back(pair):
-            q_ps = psum.tile([P, 2, M], F32, name="q_ps", tag="a")
+        def turned_sum(q):
+            turned_ps = psum.tile([P, M], F32, name="turned_ps", tag="ta")
+            for cols in blocks:
+                nc.tensor.matmul(turned_ps[:, cols], lhsT=th2_h3[:, q, cols], rhs=ident[:], is_transpose=True, start=True, stop=False)
+                nc.tensor.matmul(turned_ps[:, cols], lhsT=th3_h2[:, q, cols], rhs=ident[:], is_transpose=True, start=False, stop=True)
+            nc.scalar.copy(out=pair_turned[:, q, :], in_=turned_ps[:])
+
+        def turn_back(bank):
+            pair_ps = psum.tile([P, 2, M], F32, name="pair_ps", tag="a")
             for i in range(2):
-                for b in range(2):
-                    cols = slice(b * P, (b + 1) * P)
-                    nc.tensor.transpose(q_ps[:, i, cols], uq[:, 2 * pair + i, cols], ident[:])
-            return q_ps
+                for cols in blocks:
+                    nc.tensor.transpose(pair_ps[:, i, cols], pair_turned[:, 2 * bank + i, cols], ident[:])
+            return pair_ps
 
-        def times_h4(pair, q_ps):
-            tiles = slice(2 * pair, 2 * pair + 2)
-            nc.vector.tensor_tensor(ud[:, tiles, :], q_ps[:], h4[:, tiles, :], ALU.mult)
+        def times_h4(bank, pair_ps):
+            tiles = slice(2 * bank, 2 * bank + 2)
+            nc.vector.tensor_tensor(pair_h4[:, tiles, :], pair_ps[:], h4[:, tiles, :], ALU.mult)
 
-        fused(ub, 0, o3, h2)
+        th_times(th3_h2, 0, o3, h2)
         turned_sum(0)
-        nc.vector.quantize_mx(out=wor_q[:].bitcast(FP8X4), scales=wor_s[:], in_=wor_bf[:].rearrange("p t m j -> p (t m j)"))
-        for t in range(1, PACK):
-            fused(ua, t, o2, h3)
-            fused(ub, t, o3, h2)
-            turned_sum(t)
-        for t in range(PACK):
-            nc.scalar.activation(out=recs[:, t, :], in_=rec[:, t, :], func=ACT.Copy, scale=rs_sb[:, t:t + 1])
-        q_back = [turn_back(pair) for pair in range(2)]
-        fused(uc, 0, o4, p23)
-        fused(uc, 1, o4, p23)
-        fused(uc, 2, o4, p23)
-        times_h4(0, q_back[0])
-        fused(uc, 3, o4, p23)
-        times_h4(1, q_back[1])
+        nc.vector.quantize_mx(out=wor_q[:].bitcast(FP8X4), scales=wor_s[:], in_=wor_bf[:].rearrange("p q c j -> p (q c j)"))
+        for q in range(1, PACK):
+            th_times(th2_h3, q, o2, h3)
+            th_times(th3_h2, q, o3, h2)
+            turned_sum(q)
+        for q in range(PACK):
+            nc.scalar.activation(out=rec_rs[:, q, :], in_=rec[:, q, :], func=ACT.Copy, scale=rs_sb[:, q:q + 1])
+        pair_banks = [turn_back(bank) for bank in range(2)]
+        for q in range(PACK - 1):
+            th_times(th4_h23, q, o4, h23)
+        times_h4(0, pair_banks[0])
+        th_times(th4_h23, PACK - 1, o4, h23)
+        times_h4(1, pair_banks[1])
 
-        HM = M // 2
-        halves = [slice(0, HM), slice(HM, M)]
+        halves = [slice(0, M // 2), slice(M // 2, M)]
         weavers = [nc.scalar.copy, nc.vector.tensor_copy]
         for cols in halves:
-            nc.vector.tensor_tensor(ts[:, :, cols], ud[:, :, cols], uc[:, :, cols], ALU.add)
+            nc.vector.tensor_tensor(ts[:, :, cols], pair_h4[:, :, cols], th4_h23[:, :, cols], ALU.add)
         for cols in halves:
-            nc.vector.tensor_tensor(fo[:, :, cols], ts[:, :, cols], recs[:, :, cols], ALU.mult)
+            nc.vector.tensor_tensor(fo[:, :, cols], ts[:, :, cols], rec_rs[:, :, cols], ALU.mult)
 
         def weave(dst, src):
-            view = src[:].rearrange("p t m -> p m t")
+            view = src[:].rearrange("p q m -> p m q")
             for cols, copy in zip(halves, weavers):
                 copy(out=dst[:, cols, :], in_=view[:, cols, :])
 
         def quantise_halves(codes, scales, src):
             for cols in halves:
                 nc.vector.quantize_mx(out=codes[:, cols].bitcast(FP8X4), scales=scales[:, cols],
-                                      in_=src[:, cols, :].rearrange("p m t -> p (m t)"))
+                                      in_=src[:, cols, :].rearrange("p m q -> p (m q)"))
 
         fo_bf = sb([P, M, PACK], BF16, "fo_bf")
         weave(fo_bf, fo)
@@ -252,13 +251,13 @@ def tile_attend_ttriples_o_pl_kernel(tc, dtab_words, dtab_scales, tab_words, tab
         quantise_halves(fo_q, fo_s, fo_bf)
 
         y = sb([P, PACK, M], F32, "y")
-        out_v = out_0.rearrange("(p t) m -> p t m", t=PACK)
+        out_rows = out_0.rearrange("(p q) m -> p q m", q=PACK)
         for cols in halves:
-            yo = psum.tile([P, PACK, HM], F32, name="yo_ps", tag="a")
-            for t in range(PACK):
-                mm(yo[:, t, :], wor_q, wor_s, slice(t * P, (t + 1) * P), fo_q[:, cols], fo_s[:, cols])
+            yo = psum.tile([P, PACK, M // 2], F32, name="yo_ps", tag="a")
+            for q in range(PACK):
+                product(yo[:, q, :], wor_q, wor_s, q, fo_q[:, cols], fo_s[:, cols])
             nc.vector.tensor_tensor(y[:, :, cols], yo[:], res_sb[:, :, cols], ALU.add)
-            nc.sync.dma_start(out=out_v[:, :, cols], in_=y[:, :, cols])
+            nc.sync.dma_start(out=out_rows[:, :, cols], in_=y[:, :, cols])
 
         y_bf = sb([P, M, PACK], BF16, "y_bf")
         weave(y_bf, y)
@@ -266,6 +265,7 @@ def tile_attend_ttriples_o_pl_kernel(tc, dtab_words, dtab_scales, tab_words, tab
         y_s = sb([P, M], U8, "y_s")
         quantise_halves(y_q, y_s, y_bf)
         nc.sync.dma_start(out=words_view(out_1), in_=y_q[:].bitcast(I32))
-        for q in range(4):
-            queue = nc.scalar if q % 2 else nc.sync
-            queue.dma_start(out=out_2[0, 4 * q:4 * q + 4, :].bitcast(I32), in_=y_s[32 * q:32 * q + 4, :].bitcast(I32))
+        for quad in range(P // QUAD):
+            queue = nc.scalar if quad % 2 else nc.sync
+            queue.dma_start(out=out_2[0, 4 * quad:4 * quad + 4, :].bitcast(I32),
+                            in_=y_s[QUAD * quad:QUAD * quad + 4, :].bitcast(I32))

from contextlib import ExitStack

import concourse.mybir as mybir
from concourse.masks import make_identity

K, R, F, T, J, M = 512, 512, 512, 2048, 512, 256
FLOPS = 2 * (2 * K * R * J + R * F * M)

F32 = mybir.dt.float32
BF16 = mybir.dt.bfloat16
I32 = mybir.dt.int32
U32 = mybir.dt.uint32
U16 = mybir.dt.uint16
U8 = mybir.dt.uint8
FP8X4 = mybir.dt.float8_e4m3fn_x4
ALU = mybir.AluOpType
ACT = mybir.ActivationFunctionType

P = 128
PACK = 4
QUAD = 32
HALF_P = P // 2
W1_SCALAR_SHARE = 24
LN_FLOOR = 1e-19


def tile_attend_ttriples_o_pl_kernel(tc, dtab_words, dtab_scales, tab_words, tab_scales, w1, bias, rs, wor, res,
                                      offs, offs2, offs3, offs4, out_0, out_1, out_2):
    nc = tc.nc
    with ExitStack() as ctx:
        lists = ctx.enter_context(tc.tile_pool(name="lists", bufs=1))
        keep = ctx.enter_context(tc.tile_pool(name="keep", bufs=1))
        psum = ctx.enter_context(tc.psum_pool(name="psum", bufs=PACK))

        def sb(shape, dtype, name, after=None):
            return keep.tile(shape, dtype, name=name, tag=after or name, align_bytes=64)

        def words_view(ap):
            return ap[0].rearrange("p n q -> p (n q)").bitcast(I32)

        def product(out, lhs_codes, lhs_scales, q, rhs_codes, rhs_scales):
            cols = slice(q * P, (q + 1) * P)
            nc.tensor.matmul_mx(out=out, lhsT=lhs_codes[:, cols].bitcast(FP8X4), lhsT_scale=lhs_scales[:, cols],
                                rhs=rhs_codes.bitcast(FP8X4), rhs_scale=rhs_scales, start=True, stop=True)

        zero = sb([P, 1], F32, "zero")
        half = sb([P, 1], F32, "half")
        floor = sb([P, 1], F32, "floor")
        nc.vector.memset(zero[:], 0.0)
        nc.scalar.activation(out=half[:], in_=zero[:], func=ACT.Sigmoid)
        nc.scalar.activation(out=floor[:], in_=half[:], func=ACT.Copy, scale=2.0 * LN_FLOOR)

        tab_s = sb([P, T], U8, "tab_s")
        dtab_s = sb([P, T], U8, "dtab_s")
        nc.gpsimd.memset(dtab_s[:].bitcast(I32), 0)

        ident = sb([P, P], F32, "ident")
        make_identity(nc, ident[:])

        o1 = lists.tile([P, J // 16], U16, name="o1")
        o2 = lists.tile([P, M // 16], U16, name="o2")
        o3 = lists.tile([P, M // 16], U16, name="o3")
        o4 = lists.tile([P, M // 16], U16, name="o4")
        tab_w = sb([P, T], I32, "tab_w")
        dtab_w = sb([P, T], I32, "dtab_w")
        w1_raw = [sb([P, PACK, R // 2], F32, "w1_raw%d" % h) for h in range(2)]
        wor_raw = sb([P, PACK, F], F32, "wor_raw")
        res_sb = sb([P, PACK, M], F32, "res_sb")
        bias_sb = sb([P, PACK], F32, "bias_sb")
        rs_sb = sb([P, PACK], F32, "rs_sb")

        nc.sync.dma_start(o1[:], offs)
        for quad in range(P // QUAD):
            rows = tab_scales[0, 4 * quad:4 * quad + 4, :].bitcast(I32)
            nc.sync.dma_start(out=tab_s[QUAD * quad:QUAD * (quad + 1), :].bitcast(I32),
                              in_=rows.unsqueeze(0).broadcast_to([QUAD // 4, 4, T // 4]))
        w1_rows = w1.rearrange("(p q) r -> p q r", q=PACK)
        nc.sync.dma_start(out=w1_raw[0][:], in_=w1_rows[:, :, :R // 2])
        nc.sync.dma_start(out=tab_w[:], in_=words_view(tab_words))
        nc.sync.dma_start(out=w1_raw[1][:], in_=w1_rows[:, :, R // 2:])
        nc.sync.dma_start(out=bias_sb[:], in_=bias.rearrange("(p q) o -> p (q o)", q=PACK))
        nc.sync.dma_start(out=dtab_w[:], in_=words_view(dtab_words))
        for i in range(4):
            nc.sync.dma_start(out=dtab_s[i:P:QUAD, :].bitcast(I32), in_=dtab_scales[0, i:16:4, :].bitcast(I32))
        nc.sync.dma_start(o2[:], offs2)
        nc.sync.dma_start(o3[:], offs3)
        nc.sync.dma_start(o4[:], offs4)
        nc.sync.dma_start(out=rs_sb[:], in_=rs.rearrange("(p q) o -> p (q o)", q=PACK))
        nc.sync.dma_start(out=wor_raw[:], in_=wor.rearrange("(p q) f -> p q f", q=PACK))
        nc.sync.dma_start(out=res_sb[:], in_=res.rearrange("(p q) m -> p q m", q=PACK))

        tabg_s = sb([P, J], U8, "tabg_s")
        nc.vector.tensor_copy(tabg_s[:], tab_s[:].indirect(o1[:]))
        tabg_w = sb([P, J], U32, "tabg_w", after="tab_s")
        nc.vector.tensor_copy(tabg_w[:], tab_w[:].bitcast(U32).indirect(o1[:]))

        def deal(copy, dst, raw, c0, c1, c_first):
            copy(out=dst[:].rearrange("p q c j -> p c q j")[:, c0:c1],
                 in_=raw[:].rearrange("p j (c q) -> p c q j", q=PACK)[:, c0 - c_first:c1 - c_first])

        w1_bf = sb([P, PACK, P, PACK], BF16, "w1_bf")
        w1_q = sb([P, R], U32, "w1_q")
        w1_s = sb([P, R], U8, "w1_s")

        def quantise_w1(h):
            for q in range(PACK):
                cols = slice(q * P + HALF_P * h, q * P + HALF_P * (h + 1))
                nc.vector.quantize_mx(out=w1_q[:, cols].bitcast(FP8X4), scales=w1_s[:, cols],
                                      in_=w1_bf[:, q, HALF_P * h:HALF_P * (h + 1), :].rearrange("p c j -> p (c j)"))

        deal(nc.scalar.copy, w1_bf, w1_raw[0], 0, HALF_P, 0)
        quantise_w1(0)
        deal(nc.scalar.copy, w1_bf, w1_raw[1], HALF_P, HALF_P + W1_SCALAR_SHARE, HALF_P)
        deal(nc.vector.tensor_copy, w1_bf, w1_raw[1], HALF_P + W1_SCALAR_SHARE, P, HALF_P)
        quantise_w1(1)

        neg_bias = sb([P, PACK], F32, "neg_bias")
        nc.scalar.activation(out=neg_bias[:], in_=bias_sb[:], func=ACT.Copy, scale=-1.0)

        a_ps = []
        for q in range(PACK):
            a_q = psum.tile([P, J], F32, name="a_ps", tag="a")
            product(a_q[:], w1_q, w1_s, q, tabg_w[:], tabg_s[:])
            a_ps.append(a_q)

        dtabg_w = sb([P, J], U32, "dtabg_w", after="w1_bf")
        nc.vector.tensor_copy(dtabg_w[:], dtab_w[:].bitcast(U32).indirect(o1[:]))
        dtabg_s = sb([P, J], U8, "dtabg_s", after="dtab_w")
        nc.vector.tensor_copy(dtabg_s[:], dtab_s[:].indirect(o1[:]))
        ta_ps = []
        for q in range(PACK):
            ta_q = psum.tile([P, J], F32, name="ta_ps", tag="ta")
            product(ta_q[:], w1_q, w1_s, q, dtabg_w[:], dtabg_s[:])
            ta_ps.append(ta_q)

        sig_neg = [sb([P, J], F32, "sig_neg%d" % q) for q in range(PACK)]
        sig = sb([P, PACK, J], F32, "sig", after="dtab_s")
        ln_sig = [sb([P, J], F32, "ln_sig%d" % q) for q in range(PACK)]
        soft = [sb([P, J], F32, "soft%d" % q) for q in range(PACK)]
        th1 = [sb([P, J], F32, "th1_%d" % q) for q in range(PACK)]
        for q in range(PACK):
            nc.scalar.activation(out=sig_neg[q][:], in_=a_ps[q][:], func=ACT.Sigmoid, bias=neg_bias[:, q:q + 1], scale=-1.0)
        for q in range(PACK):
            nc.vector.tensor_scalar(sig[:, q, :], sig_neg[q][:], -1.0, 1.0, ALU.mult, ALU.add)
        for q in range(PACK):
            nc.scalar.activation(out=ln_sig[q][:], in_=sig_neg[q][:], func=ACT.Ln, bias=floor[:])
            nc.scalar.activation(out=soft[q][:], in_=ln_sig[q][:], func=ACT.Copy, scale=-1.0)
        for q in range(PACK):
            nc.vector.tensor_tensor(th1[q][:], ta_ps[q][:], sig[:, q, :], ALU.mult)

        h1 = [sb([P, J], F32, "h1_%d" % q, after="dtab_s" if q == 0 else None) for q in range(PACK)]
        wor_bf = sb([P, PACK, P, PACK], BF16, "wor_bf", after="ln_sig%d" % (PACK - 1))
        deal(nc.scalar.copy, wor_bf, wor_raw, 0, P, 0)
        wor_q = sb([P, F], U32, "wor_q")
        wor_s = sb([P, F], U8, "wor_s")

        h2 = sb([P, PACK, M], F32, "h2")
        h3 = sb([P, PACK, M], F32, "h3")
        h4 = sb([P, PACK, M], F32, "h4")
        h23 = sb([P, PACK, M], F32, "h23")
        s = sb([P, PACK, M], F32, "s")

        def softplus(q):
            nc.vector.scalar_tensor_tensor(h1[q][:], a_ps[q][:], bias_sb[:, q:q + 1], soft[q][:], ALU.add, ALU.max)

        softplus(0)
        for q in range(PACK):
            nc.vector.tensor_copy(h2[:, q, :], h1[q][:].indirect(o2[:]))
            nc.vector.tensor_copy(h3[:, q, :], h1[q][:].indirect(o3[:]))
            if q + 1 < PACK:
                softplus(q + 1)
            nc.vector.tensor_copy(h4[:, q, :], h1[q][:].indirect(o4[:]))

        th2_h3 = sb([P, PACK, M], F32, "th2_h3")
        th3_h2 = sb([P, PACK, M], F32, "th3_h2")
        th4_h23 = sb([P, PACK, M], F32, "th4_h23")
        pair_h4 = sb([P, PACK, M], F32, "pair_h4")
        ts = sb([P, PACK, M], F32, "ts")
        fo = sb([P, PACK, M], F32, "fo")
        ln_den = sb([P, PACK, M], F32, "ln_den")
        rec = sb([P, PACK, M], F32, "rec")
        rec_rs = sb([P, PACK, M], F32, "rec_rs")

        def th_times(out, q, offsets, other):
            nc.vector.tensor_tensor(out[:, q, :], th1[q][:].indirect(offsets[:]), other[:, q, :], ALU.mult)

        nc.vector.tensor_tensor(h23[:], h2[:], h3[:], ALU.mult)
        th_times(th2_h3, 0, o2, h3)
        nc.vector.tensor_tensor(s[:], h23[:], h4[:], ALU.mult)
        nc.scalar.activation(out=ln_den[:], in_=s[:], func=ACT.Ln, bias=1.0)
        nc.scalar.activation(out=rec[:], in_=ln_den[:], func=ACT.Exp, scale=-1.0)

        pair_turned = sb([P, PACK, M], F32, "pair_turned", after="ln_den")
        blocks = [slice(b * P, (b + 1) * P) for b in range(M // P)]

        def turned_sum(q):
            turned_ps = psum.tile([P, M], F32, name="turned_ps", tag="ta")
            for cols in blocks:
                nc.tensor.matmul(turned_ps[:, cols], lhsT=th2_h3[:, q, cols], rhs=ident[:], is_transpose=True, start=True, stop=False)
                nc.tensor.matmul(turned_ps[:, cols], lhsT=th3_h2[:, q, cols], rhs=ident[:], is_transpose=True, start=False, stop=True)
            nc.scalar.copy(out=pair_turned[:, q, :], in_=turned_ps[:])

        def turn_back(bank):
            pair_ps = psum.tile([P, 2, M], F32, name="pair_ps", tag="a")
            for i in range(2):
                for cols in blocks:
                    nc.tensor.transpose(pair_ps[:, i, cols], pair_turned[:, 2 * bank + i, cols], ident[:])
            return pair_ps

        def times_h4(bank, pair_ps):
            tiles = slice(2 * bank, 2 * bank + 2)
            nc.vector.tensor_tensor(pair_h4[:, tiles, :], pair_ps[:], h4[:, tiles, :], ALU.mult)

        th_times(th3_h2, 0, o3, h2)
        turned_sum(0)
        nc.vector.quantize_mx(out=wor_q[:].bitcast(FP8X4), scales=wor_s[:], in_=wor_bf[:].rearrange("p q c j -> p (q c j)"))
        for q in range(1, PACK):
            th_times(th2_h3, q, o2, h3)
            th_times(th3_h2, q, o3, h2)
            turned_sum(q)
        for q in range(PACK):
            nc.scalar.activation(out=rec_rs[:, q, :], in_=rec[:, q, :], func=ACT.Copy, scale=rs_sb[:, q:q + 1])
        pair_banks = [turn_back(bank) for bank in range(2)]
        for q in range(PACK - 1):
            th_times(th4_h23, q, o4, h23)
        times_h4(0, pair_banks[0])
        th_times(th4_h23, PACK - 1, o4, h23)
        times_h4(1, pair_banks[1])

        halves = [slice(0, M // 2), slice(M // 2, M)]
        weavers = [nc.scalar.copy, nc.vector.tensor_copy]
        for cols in halves:
            nc.vector.tensor_tensor(ts[:, :, cols], pair_h4[:, :, cols], th4_h23[:, :, cols], ALU.add)
        for cols in halves:
            nc.vector.tensor_tensor(fo[:, :, cols], ts[:, :, cols], rec_rs[:, :, cols], ALU.mult)

        def weave(dst, src):
            view = src[:].rearrange("p q m -> p m q")
            for cols, copy in zip(halves, weavers):
                copy(out=dst[:, cols, :], in_=view[:, cols, :])

        def quantise_halves(codes, scales, src):
            for cols in halves:
                nc.vector.quantize_mx(out=codes[:, cols].bitcast(FP8X4), scales=scales[:, cols],
                                      in_=src[:, cols, :].rearrange("p m q -> p (m q)"))

        fo_bf = sb([P, M, PACK], BF16, "fo_bf")
        weave(fo_bf, fo)
        fo_q = sb([P, M], U32, "fo_q")
        fo_s = sb([P, M], U8, "fo_s")
        quantise_halves(fo_q, fo_s, fo_bf)

        y = sb([P, PACK, M], F32, "y")
        out_rows = out_0.rearrange("(p q) m -> p q m", q=PACK)
        for cols in halves:
            yo = psum.tile([P, PACK, M // 2], F32, name="yo_ps", tag="a")
            for q in range(PACK):
                product(yo[:, q, :], wor_q, wor_s, q, fo_q[:, cols], fo_s[:, cols])
            nc.vector.tensor_tensor(y[:, :, cols], yo[:], res_sb[:, :, cols], ALU.add)
            nc.sync.dma_start(out=out_rows[:, :, cols], in_=y[:, :, cols])

        y_bf = sb([P, M, PACK], BF16, "y_bf")
        weave(y_bf, y)
        y_q = sb([P, M], U32, "y_q")
        y_s = sb([P, M], U8, "y_s")
        quantise_halves(y_q, y_s, y_bf)
        nc.sync.dma_start(out=words_view(out_1), in_=y_q[:].bitcast(I32))
        for quad in range(P // QUAD):
            queue = nc.scalar if quad % 2 else nc.sync
            queue.dma_start(out=out_2[0, 4 * quad:4 * quad + 4, :].bitcast(I32),
                            in_=y_s[QUAD * quad:QUAD * quad + 4, :].bitcast(I32))
